import numpy as np
import ml_dtypes


def mxq(x, axis, fmt="e4m3"):
    dtype, down = {"e4m3": (ml_dtypes.float8_e4m3fn, 7), "e5m2": (ml_dtypes.float8_e5m2, 14)}[fmt]
    v = np.moveaxis(np.asarray(x, np.float32).astype(ml_dtypes.bfloat16).astype(np.float64), axis, -1)
    blocks = v.reshape(v.shape[:-1] + (-1, 32))
    amax = np.abs(blocks).max(-1, keepdims=True)
    byte = np.maximum(np.where(amax > 0, np.frexp(amax)[1] - 1 + 127, 0) - down, 1)
    scale = np.exp2(byte - 127.0)
    codes = (blocks / scale).astype(np.float32).astype(dtype).astype(np.float64)
    return np.moveaxis((codes * scale).reshape(v.shape), -1, axis)


WIDE = False


def mx_kscale(k):
    if not WIDE:
        return np.ones(k)
    levels = np.array([10, -10, 5, -5, 0])
    if k % 512:
        return np.exp2(np.random.permutation(np.resize(levels, k // 32))).repeat(32)
    a = np.empty((k // 512, 16))
    for p in range(k // 512):
        a[p, :8] = np.random.permutation(np.resize(levels, 8))
        for g in range(8):
            far = levels[np.abs(levels - a[p, g]) >= 10]
            a[p, g + 8] = far[np.random.randint(len(far))]
    return np.exp2(a.ravel()).repeat(32)


def f64(x):
    return np.asarray(x).astype(np.float64)


def striped(idx):
    return np.tile(idx.reshape(-1, 16).T, (8, 1)).astype(np.uint16)


def unstriped(offs):
    return offs[:16].T.reshape(-1).astype(np.int64)


def silu(v):
    return v / (1.0 + np.exp(-np.maximum(v, -700.0)))


K, T, E, C, H, N = 1024, 1536, 6, 128, 512, 128


def by_expert(wq, xq):
    return np.concatenate([wq[e].T @ xq[:, e * C:(e + 1) * C] for e in range(E)], axis=1)


def setup_inputs():
    n = np.random.standard_normal
    s = mx_kscale(K)[:, None]
    u = mx_kscale(H)
    return {
        "xT": (n((K, T)) * s).astype(np.float32),
        "w1": (n((E, K, H)) / np.sqrt(K) / s[None]).astype(np.float32),
        "w3": (n((E, K, H)) / np.sqrt(K) / s[None] * u[None, None, :]).astype(np.float32),
        "w2": (n((E, H, N)) / np.sqrt(H) / u[None, :, None]).astype(np.float32),
        "gate": np.tile(np.random.uniform(0.2, 1.0, E * C), (N, 1)).astype(np.float32),
        "offs": striped(np.random.permutation(T)[:E * C]),
    }


def reference(xT, w1, w3, w2, gate, offs):
    idx = unstriped(offs)
    xq = mxq(f64(xT)[:, idx], 0, "e4m3")
    h = silu(by_expert(mxq(f64(w1), 1, "e4m3"), xq))
    h = h * by_expert(mxq(f64(w3), 1, "e4m3"), xq)
    y = by_expert(mxq(f64(w2), 1, "e4m3"), mxq(h, 0, "e4m3"))
    out = np.zeros((N, T))
    out[:, idx] = f64(gate) * y
    return out

@@ -1,0 +1,254 @@
+from contextlib import ExitStack
+
+import concourse.mybir as mybir
+
+K, T, E, C, H, N = 1024, 1536, 6, 128, 512, 128
+S = E * C
+FLOPS = 2 * (2 * S * K * H) + 2 * S * H * N
+
+F32 = mybir.dt.float32
+BF16 = mybir.dt.bfloat16
+U32 = mybir.dt.uint32
+U16 = mybir.dt.uint16
+U8 = mybir.dt.uint8
+FP8X4 = mybir.dt.float8_e4m3fn_x4
+SILU = mybir.ActivationFunctionType.Silu
+MULT = mybir.AluOpType.mult
+
+P = 128
+J = 4
+KP = P * J
+G = K // KP
+XB = 512
+
+
+def tile_routed_moe_kernel(tc, xT, w1, w3, w2, gate, offs, out):
+    nc = tc.nc
+    with ExitStack() as ctx:
+        keep = ctx.enter_context(tc.tile_pool(name="keep", bufs=1))
+        ring = ctx.enter_context(tc.tile_pool(name="ring", bufs=8))
+        two = ctx.enter_context(tc.tile_pool(name="two", bufs=2))
+        three = ctx.enter_context(tc.tile_pool(name="three", bufs=3))
+        four = ctx.enter_context(tc.tile_pool(name="four", bufs=4))
+        psum = ctx.enter_context(tc.psum_pool(name="psum", bufs=2))
+
+        offsets = keep.tile([P, S // 16], U16, name="offsets")
+        window = keep.tile([P, T], F32, name="window")
+        y_all = keep.tile([P, S], F32, name="y_all")
+        gates = keep.tile([P, S], F32, name="gates")
+        warm = keep.tile([P, 8], F32, name="warm")
+
+        nc.gpsimd.memset(warm[:], 0.0)
+        nc.gpsimd.memset(window[:], 0.0)
+        nc.scalar.activation(warm[:, 0:1], warm[:, 1:2], SILU)
+
+        raw, grp, codes, scales = {}, {}, {}, {}
+        acc, act, hid, hcode, hscale, gc, gs = {}, {}, {}, {}, {}, {}, {}
+        weight = {1: w1, 3: w3}
+
+        def load_w(l, e, g):
+            r = ring.tile([P, J * H], F32, name="raw", tag="raw")
+            nc.sync.dma_start(r[:], weight[l][e, g * KP:(g + 1) * KP, :].rearrange("(p j) c -> p (j c)", j=J))
+            raw[l, e, g] = r
+
+        def load_w2(e):
+            pool, tag = (two, "w2raw") if e < E - 1 else (ring, "raw")
+            r = pool.tile([P, J * N], F32, name=tag, tag=tag)
+            nc.sync.dma_start(r[:], w2[e].rearrange("(p j) n -> p (j n)", j=J))
+            raw[2, e] = r
+
+        def load_x(g):
+            r = keep.tile([P, J * T], F32, name="xraw%d" % g)
+            nc.sync.dma_start(r[:], xT[g * KP:(g + 1) * KP, :].rearrange("(p j) n -> p (j n)", j=J))
+            raw["x", g] = r
+
+        def copy(eng, dst, src):
+            if eng == "v":
+                nc.vector.tensor_copy(out=dst, in_=src)
+            else:
+                nc.scalar.copy(dst, src)
+
+        def quant(code, scale, src):
+            nc.vector.quantize_mx(out=code.bitcast(FP8X4), scales=scale, in_=src)
+
+        def cw(eng, l, e, g):
+            t = four.tile([P, J * H], BF16, name="wgrp", tag="wgrp", align_bytes=64)
+            grp[l, e, g] = t
+            dst = t[:].rearrange("p (t m j) -> p m j t", t=J, j=J)
+            src = raw[l, e, g][:].rearrange("p (j m t) -> p m j t", j=J, t=J)
+            if len(eng) == 1:
+                copy(eng, dst, src)
+            else:
+                for h in range(2):
+                    copy(eng[h], dst[:, :, :, 2 * h:2 * h + 2], src[:, :, :, 2 * h:2 * h + 2])
+
+        def qw(l, e, g, parts=1):
+            tag = "%d%d" % (l, g)
+            code = three.tile([P, H], U32, name="c" + tag, tag="c" + tag, align_bytes=64)
+            scale = three.tile([P, H], U8, name="s" + tag, tag="s" + tag, align_bytes=64)
+            n = H // parts
+            for h in range(parts):
+                cs = slice(h * n, (h + 1) * n)
+                quant(code[:, cs], scale[:, cs], grp[l, e, g][:, h * J * n:(h + 1) * J * n])
+            codes[l, e, g], scales[l, e, g] = code, scale
+
+        def cw2(eng, e):
+            t = two.tile([P, N, J], BF16, name="w2grp", tag="w2grp", align_bytes=64)
+            copy(eng, t[:].rearrange("p (c i) j -> p c j i", i=4), raw[2, e][:].rearrange("p (j c i) -> p c j i", j=J, i=4))
+            grp[2, e] = t
+
+        def qw2(e):
+            code = two.tile([P, N], U32, name="c2", tag="c2", align_bytes=64)
+            scale = two.tile([P, N], U8, name="s2", tag="s2", align_bytes=64)
+            quant(code[:], scale[:], grp[2, e][:].rearrange("p n j -> p (n j)"))
+            codes[2, e], scales[2, e] = code, scale
+
+        def cx(eng, g, b):
+            cols = slice(b * XB, (b + 1) * XB)
+            t = three.tile([P, XB, J], BF16, name="xgrp", tag="xgrp", align_bytes=64)
+            rows = raw["x", g][:].rearrange("p (j n) -> p j n", j=J)
+            copy(eng, t[:].rearrange("p (c i) j -> p c j i", i=4), rows[:, :, cols].rearrange("p j (c i) -> p c j i", i=4))
+            grp["x", g, b] = t
+
+        def qx(g, b):
+            cols = slice(b * XB, (b + 1) * XB)
+            quant(xcode[g][:, cols], xscale[g][:, cols], grp["x", g, b][:].rearrange("p n j -> p (n j)"))
+
+        xcode = [keep.tile([P, T], U32, name="xc%d" % g, align_bytes=64) for g in range(G)]
+        xscale = [keep.tile([P, T], U8, name="xs%d" % g, align_bytes=64) for g in range(G)]
+
+        def gather(g):
+            gc[g] = keep.tile([P, S], U32, name="gc%d" % g, align_bytes=64)
+            gs[g] = keep.tile([P, S], U8, name="gs%d" % g, align_bytes=64)
+            nc.vector.tensor_copy(gc[g][:], xcode[g][:].indirect(offsets[:]))
+            nc.vector.tensor_copy(gs[g][:], xscale[g][:].indirect(offsets[:]))
+
+        def mm(l, e):
+            a = psum.tile([P, J, C], F32, name="acc%d" % l, tag="acc%d" % l)
+            cols = slice(e * C, (e + 1) * C)
+            for t in range(J):
+                for g in range(G):
+                    nc.tensor.matmul_mx(
+                        out=a[:, t, :],
+                        lhsT=codes[l, e, g][:, t * P:(t + 1) * P].bitcast(FP8X4),
+                        lhsT_scale=scales[l, e, g][:, t * P:(t + 1) * P],
+                        rhs=gc[g][:, cols].bitcast(FP8X4),
+                        rhs_scale=gs[g][:, cols],
+                        start=(g == 0),
+                        stop=(g == G - 1),
+                    )
+            acc[l, e] = a
+
+        def silu(e):
+            act[e] = two.tile([P, J, C], F32, name="act")
+            nc.scalar.activation(act[e][:], acc[1, e][:], SILU)
+
+        def mul(e):
+            hid[e] = two.tile([P, C, J], BF16, name="hid", align_bytes=64)
+            nc.vector.tensor_tensor(hid[e][:], acc[3, e][:].rearrange("p t n -> p n t"), act[e][:].rearrange("p t n -> p n t"), MULT)
+
+        def qh(e):
+            hcode[e] = two.tile([P, C], U32, name="hc", align_bytes=64)
+            hscale[e] = two.tile([P, C], U8, name="hs", align_bytes=64)
+            quant(hcode[e][:], hscale[e][:], hid[e][:].rearrange("p n t -> p (n t)"))
+
+        def my(e):
+            a = psum.tile([P, C], F32, name="accy")
+            nc.tensor.matmul_mx(out=a[:], lhsT=codes[2, e][:].bitcast(FP8X4), lhsT_scale=scales[2, e][:],
+                                rhs=hcode[e][:].bitcast(FP8X4), rhs_scale=hscale[e][:], start=True, stop=True)
+            acc["y", e] = a
+
+        def cy(eng, e):
+            copy(eng, y_all[:, e * C:(e + 1) * C], acc["y", e][:])
+
+        def scatter(a, b):
+            nc.vector.tensor_tensor(window[:].indirect(offsets[:, a // 16:b // 16]), y_all[:, a:b], gates[:, a:b], MULT)
+
+        load_w(1, 0, 0)
+        load_w(1, 0, 1)
+        load_x(0)
+        nc.sync.dma_start(offsets[:], offs)
+        load_w(3, 0, 0)
+        load_x(1)
+
+        cw("s", 1, 0, 0)
+        cw("v", 1, 0, 1)
+        qw(1, 0, 0)
+        qw(1, 0, 1)
+        cx("v", 0, 0)
+        cx("s", 0, 1)
+        qx(0, 0)
+        cx("v", 0, 2)
+        qx(0, 1)
+        qx(0, 2)
+        gather(0)
+        cw("s", 3, 0, 0)
+        cx("s", 1, 0)
+        cx("v", 1, 1)
+        qw(3, 0, 0)
+        cx("s", 1, 2)
+        qx(1, 0)
+        qx(1, 1)
+        qx(1, 2)
+        load_w(3, 0, 1)
+        load_w(1, 1, 0)
+        cw("v", 3, 0, 1)
+        gather(1)
+        qw(3, 0, 1)
+        load_w2(0)
+        cw2("s", 0)
+        cw("s", 1, 1, 0)
+        mm(1, 0)
+        silu(0)
+        mm(3, 0)
+        qw2(0)
+        nc.sync.dma_start(gates[:], gate)
+
+        for e in range(1, E):
+            last = e == E - 1
+            load_w(1, e, 1)
+            if not last:
+                load_w2(e)
+            load_w(3, e, 0)
+            load_w(3, e, 1)
+            if last:
+                load_w2(e)
+            else:
+                load_w(1, e + 1, 0)
+            cw("v", 1, e, 1)
+            cw("s", 3, e, 0)
+            qw(1, e, 0)
+            mul(e - 1)
+            qw(1, e, 1)
+            mm(1, e)
+            qh(e - 1)
+            my(e - 1)
+            cy("s", e - 1)
+            silu(e)
+            if e == 4:
+                scatter(0, 384)
+            if e == 5:
+                scatter(384, 576)
+            if not last:
+                cw2("s", e)
+            if last:
+                cw("vs", 3, e, 1)
+                qw(3, e, 0)
+                qw(3, e, 1, 2)
+                cw2("s", e)
+                qw2(e)
+            else:
+                extra = "s" if e == 2 else "v"
+                cw(extra, 3, e, 1)
+                qw(3, e, 0)
+                qw(3, e, 1)
+                cw("s", 1, e + 1, 0)
+                qw2(e)
+            mm(3, e)
+        e = E - 1
+        mul(e)
+        qh(e)
+        my(e)
+        cy("s", e)
+        scatter(576, 768)
+        nc.sync.dma_start(out, window[:])

@@ -15,6 +15,143 @@ FP8X4 = mybir.dt.float8_e4m3fn_x4
 SILU = mybir.ActivationFunctionType.Silu
 MULT = mybir.AluOpType.mult
 
+LOADS_AND_STEPS = [
+    ('lw', 1, 0, 0),
+    ('cw', 's', 1, 0, 0),
+    ('lo',),
+    ('l2', 0),
+    ('c2', 'v', 0),
+    ('q2', 0),
+    ('lx', 0),
+    ('cx', 's', 0, 0),
+    ('cx', 'v', 0, 1),
+    ('cx', 'v', 0, 2),
+    ('qx', 0, 0),
+    ('qx', 0, 1),
+    ('qx', 0, 2),
+    ('ga', 0),
+    ('lw', 1, 0, 1),
+    ('cw', 'vs', 1, 0, 1),
+    ('qw', 1, 0),
+    ('lx', 1),
+    ('cx', 's', 1, 0),
+    ('cx', 'v', 1, 1),
+    ('cx', 's', 1, 2),
+    ('qx', 1, 0),
+    ('qx', 1, 1),
+    ('qx', 1, 2),
+    ('ga', 1),
+    ('mm', 1, 0),
+    ('silu', 0),
+    ('lw', 3, 0, 0),
+    ('cw', 'vs', 3, 0, 0),
+    ('lw', 1, 1, 0),
+    ('cw', 's', 1, 1, 0),
+    ('lw', 3, 1, 0),
+    ('cw', 'sv', 3, 1, 0),
+    ('lw', 1, 1, 1),
+    ('cw', 'v', 1, 1, 1),
+    ('qw', 1, 1),
+    ('lw', 3, 0, 1),
+    ('cw', 'v', 3, 0, 1),
+    ('qw', 3, 0),
+    ('mm', 3, 0),
+    ('mm', 1, 1),
+    ('silu', 1),
+    ('lw', 3, 1, 1),
+    ('cw', 'vs', 3, 1, 1),
+    ('qw', 3, 1),
+    ('mm', 3, 1),
+    ('lg',),
+    ('lw', 1, 2, 0),
+    ('cw', 's', 1, 2, 0),
+    ('lw', 1, 2, 1),
+    ('cw', 's', 1, 2, 1),
+    ('qw', 1, 2),
+    ('mm', 1, 2),
+    ('silu', 2),
+    ('l2', 1),
+    ('c2', 's', 1),
+    ('q2', 1),
+    ('mul', 0, 0, 2),
+    ('mul', 1, 1, 2),
+    ('qh', (0, 1)),
+    ('my', (0, 1)),
+    ('cy', 's', (0, 1)),
+    ('sc', 0, 256),
+    ('lw', 3, 2, 0),
+    ('cw', 's', 3, 2, 0),
+    ('l2', 2),
+    ('c2', 'v', 2),
+    ('q2', 2),
+    ('lw', 3, 2, 1),
+    ('cw', 'v', 3, 2, 1),
+    ('qw', 3, 2),
+    ('mm', 3, 2),
+    ('lw', 1, 3, 0),
+    ('cw', 'v', 1, 3, 0),
+    ('lw', 1, 3, 1),
+    ('cw', 's', 1, 3, 1),
+    ('qw', 1, 3),
+    ('mm', 1, 3),
+    ('silu', 3),
+    ('lw', 3, 3, 0),
+    ('cw', 's', 3, 3, 0),
+    ('lw', 3, 3, 1),
+    ('cw', 'v', 3, 3, 1),
+    ('qw', 3, 3),
+    ('mm', 3, 3),
+    ('lw', 1, 4, 0),
+    ('cw', 'vs', 1, 4, 0),
+    ('l2', 3),
+    ('c2', 'v', 3),
+    ('q2', 3),
+    ('mul', 2, 0, 2),
+    ('mul', 3, 1, 2),
+    ('qh', (2, 3)),
+    ('my', (2, 3)),
+    ('cy', 's', (2, 3)),
+    ('sc', 256, 512),
+    ('lw', 1, 4, 1),
+    ('cw', 'sv', 1, 4, 1),
+    ('qw', 1, 4),
+    ('mm', 1, 4),
+    ('silu', 4),
+    ('lw', 3, 4, 0),
+    ('cw', 's', 3, 4, 0),
+    ('lw', 3, 4, 1),
+    ('cw', 'v', 3, 4, 1),
+    ('qw', 3, 4),
+    ('mm', 3, 4),
+    ('l2', 4),
+    ('c2', 'v', 4),
+    ('q2', 4),
+    ('lw', 3, 5, 0),
+    ('cw', 'v', 3, 5, 0),
+    ('qw', 3, 5, 0, 512),
+    ('lw', 1, 5, 0),
+    ('cw', 's', 1, 5, 0),
+    ('lw', 1, 5, 1),
+    ('cw', 'v', 1, 5, 1),
+    ('qw', 1, 5),
+    ('mm', 1, 5),
+    ('silu', 5),
+    ('lw', 3, 5, 1),
+    ('cw', 'vs', 3, 5, 1),
+    ('qw', 3, 5, 512, 768),
+    ('qw', 3, 5, 768, 1024),
+    ('mm', 3, 5),
+    ('l2', 5, 'ring'),
+    ('c2', 's', 5),
+    ('q2', 5),
+    ('mul', 4, 0, 2),
+    ('mul', 5, 1, 2),
+    ('qh', (4, 5)),
+    ('my', (4, 5)),
+    ('cy', 'v', (4, 5)),
+    ('sc', 512, 768),
+]
+
 P = 128
 J = 4
 KP = P * J
@@ -26,10 +163,11 @@ def tile_routed_moe_kernel(tc, xT, w1, w3, w2, gate, offs, out):
     nc = tc.nc
     with ExitStack() as ctx:
         keep = ctx.enter_context(tc.tile_pool(name="keep", bufs=1))
-        ring = ctx.enter_context(tc.tile_pool(name="ring", bufs=8))
+        ring = ctx.enter_context(tc.tile_pool(name="ring", bufs=7))
         two = ctx.enter_context(tc.tile_pool(name="two", bufs=2))
         three = ctx.enter_context(tc.tile_pool(name="three", bufs=3))
-        four = ctx.enter_context(tc.tile_pool(name="four", bufs=4))
+        pair = ctx.enter_context(tc.tile_pool(name="pair", bufs=2))
+        cpool = ctx.enter_context(tc.tile_pool(name="cpool", bufs=2))
         psum = ctx.enter_context(tc.psum_pool(name="psum", bufs=2))
 
         offsets = keep.tile([P, S // 16], U16, name="offsets")
@@ -51,15 +189,17 @@ def tile_routed_moe_kernel(tc, xT, w1, w3, w2, gate, offs, out):
             nc.sync.dma_start(r[:], weight[l][e, g * KP:(g + 1) * KP, :].rearrange("(p j) c -> p (j c)", j=J))
             raw[l, e, g] = r
 
-        def load_w2(e):
-            pool, tag = (two, "w2raw") if e < E - 1 else (ring, "raw")
+        def load_w2(e, pool_name="two"):
+            pool, tag = (two, "w2raw") if pool_name == "two" else (ring, "raw")
             r = pool.tile([P, J * N], F32, name=tag, tag=tag)
             nc.sync.dma_start(r[:], w2[e].rearrange("(p j) n -> p (j n)", j=J))
             raw[2, e] = r
 
         def load_x(g):
             r = keep.tile([P, J * T], F32, name="xraw%d" % g)
-            nc.sync.dma_start(r[:], xT[g * KP:(g + 1) * KP, :].rearrange("(p j) n -> p (j n)", j=J))
+            rows = xT[g * KP:(g + 1) * KP, :].rearrange("(p j) n -> p j n", j=J)
+            for j in range(J):
+                nc.sync.dma_start(r[:, j * T:(j + 1) * T], rows[:, j, :])
             raw["x", g] = r
 
         def copy(eng, dst, src):
@@ -72,9 +212,10 @@ def tile_routed_moe_kernel(tc, xT, w1, w3, w2, gate, offs, out):
             nc.vector.quantize_mx(out=code.bitcast(FP8X4), scales=scale, in_=src)
 
         def cw(eng, l, e, g):
-            t = four.tile([P, J * H], BF16, name="wgrp", tag="wgrp", align_bytes=64)
-            grp[l, e, g] = t
-            dst = t[:].rearrange("p (t m j) -> p m j t", t=J, j=J)
+            if g == 0:
+                grp[l, e] = pair.tile([P, G * J * H], BF16, name="wgrp", tag="wgrp", align_bytes=64)
+            t = grp[l, e][:, g * J * H:(g + 1) * J * H]
+            dst = t.rearrange("p (t m j) -> p m j t", t=J, j=J)
             src = raw[l, e, g][:].rearrange("p (j m t) -> p m j t", j=J, t=J)
             if len(eng) == 1:
                 copy(eng, dst, src)
@@ -82,15 +223,11 @@ def tile_routed_moe_kernel(tc, xT, w1, w3, w2, gate, offs, out):
                 for h in range(2):
                     copy(eng[h], dst[:, :, :, 2 * h:2 * h + 2], src[:, :, :, 2 * h:2 * h + 2])
 
-        def qw(l, e, g, parts=1):
-            tag = "%d%d" % (l, g)
-            code = three.tile([P, H], U32, name="c" + tag, tag="c" + tag, align_bytes=64)
-            scale = three.tile([P, H], U8, name="s" + tag, tag="s" + tag, align_bytes=64)
-            n = H // parts
-            for h in range(parts):
-                cs = slice(h * n, (h + 1) * n)
-                quant(code[:, cs], scale[:, cs], grp[l, e, g][:, h * J * n:(h + 1) * J * n])
-            codes[l, e, g], scales[l, e, g] = code, scale
+        def qw(l, e, a=0, b=G * H):
+            if a == 0:
+                codes[l, e] = cpool.tile([P, G * H], U32, name="c%d" % l, tag="c%d" % l, align_bytes=64)
+                scales[l, e] = cpool.tile([P, G * H], U8, name="s%d" % l, tag="s%d" % l, align_bytes=64)
+            quant(codes[l, e][:, a:b], scales[l, e][:, a:b], grp[l, e][:, J * a:J * b])
 
         def cw2(eng, e):
             t = two.tile([P, N, J], BF16, name="w2grp", tag="w2grp", align_bytes=64)
@@ -98,8 +235,8 @@ def tile_routed_moe_kernel(tc, xT, w1, w3, w2, gate, offs, out):
             grp[2, e] = t
 
         def qw2(e):
-            code = two.tile([P, N], U32, name="c2", tag="c2", align_bytes=64)
-            scale = two.tile([P, N], U8, name="s2", tag="s2", align_bytes=64)
+            code = three.tile([P, N], U32, name="c2", tag="c2", align_bytes=64)
+            scale = three.tile([P, N], U8, name="s2", tag="s2", align_bytes=64)
             quant(code[:], scale[:], grp[2, e][:].rearrange("p n j -> p (n j)"))
             codes[2, e], scales[2, e] = code, scale
 
@@ -130,8 +267,8 @@ def tile_routed_moe_kernel(tc, xT, w1, w3, w2, gate, offs, out):
                 for g in range(G):
                     nc.tensor.matmul_mx(
                         out=a[:, t, :],
-                        lhsT=codes[l, e, g][:, t * P:(t + 1) * P].bitcast(FP8X4),
-                        lhsT_scale=scales[l, e, g][:, t * P:(t + 1) * P],
+                        lhsT=codes[l, e][:, g * H + t * P:g * H + (t + 1) * P].bitcast(FP8X4),
+                        lhsT_scale=scales[l, e][:, g * H + t * P:g * H + (t + 1) * P],
                         rhs=gc[g][:, cols].bitcast(FP8X4),
                         rhs_scale=gs[g][:, cols],
                         start=(g == 0),
@@ -143,112 +280,72 @@ def tile_routed_moe_kernel(tc, xT, w1, w3, w2, gate, offs, out):
             act[e] = two.tile([P, J, C], F32, name="act")
             nc.scalar.activation(act[e][:], acc[1, e][:], SILU)
 
-        def mul(e):
-            hid[e] = two.tile([P, C, J], BF16, name="hid", align_bytes=64)
-            nc.vector.tensor_tensor(hid[e][:], acc[3, e][:].rearrange("p t n -> p n t"), act[e][:].rearrange("p t n -> p n t"), MULT)
+        def mul(e, i, n):
+            if i == 0:
+                hid[e] = two.tile([P, n * C, J], BF16, name="hid%d" % n, tag="hid%d" % n, align_bytes=64)
+                hid["n"] = hid[e]
+            h = hid["n"][:, i * C:(i + 1) * C, :]
+            nc.vector.tensor_tensor(h, acc[3, e][:].rearrange("p t n -> p n t"), act[e][:].rearrange("p t n -> p n t"), MULT)
 
-        def qh(e):
-            hcode[e] = two.tile([P, C], U32, name="hc", align_bytes=64)
-            hscale[e] = two.tile([P, C], U8, name="hs", align_bytes=64)
-            quant(hcode[e][:], hscale[e][:], hid[e][:].rearrange("p n t -> p (n t)"))
+        def qh(es):
+            n = len(es)
+            hcode[es] = two.tile([P, n * C], U32, name="hc%d" % n, tag="hc%d" % n, align_bytes=64)
+            hscale[es] = two.tile([P, n * C], U8, name="hs%d" % n, tag="hs%d" % n, align_bytes=64)
+            quant(hcode[es][:], hscale[es][:], hid["n"][:].rearrange("p n t -> p (n t)"))
 
-        def my(e):
-            a = psum.tile([P, C], F32, name="accy")
-            nc.tensor.matmul_mx(out=a[:], lhsT=codes[2, e][:].bitcast(FP8X4), lhsT_scale=scales[2, e][:],
-                                rhs=hcode[e][:].bitcast(FP8X4), rhs_scale=hscale[e][:], start=True, stop=True)
-            acc["y", e] = a
+        def my(es):
+            n = len(es)
+            a = psum.tile([P, n * C], F32, name="accy", tag="accy")
+            for i, e in enumerate(es):
+                cols = slice(i * C, (i + 1) * C)
+                nc.tensor.matmul_mx(out=a[:, cols], lhsT=codes[2, e][:].bitcast(FP8X4), lhsT_scale=scales[2, e][:],
+                                    rhs=hcode[es][:, cols].bitcast(FP8X4), rhs_scale=hscale[es][:, cols], start=True, stop=True)
+            acc["y", es] = a
 
-        def cy(eng, e):
-            copy(eng, y_all[:, e * C:(e + 1) * C], acc["y", e][:])
+        def cy(eng, es):
+            copy(eng, y_all[:, es[0] * C:(es[-1] + 1) * C], acc["y", es][:])
 
         def scatter(a, b):
             nc.vector.tensor_tensor(window[:].indirect(offsets[:, a // 16:b // 16]), y_all[:, a:b], gates[:, a:b], MULT)
 
-        load_w(1, 0, 0)
-        load_w(1, 0, 1)
-        load_x(0)
-        nc.sync.dma_start(offsets[:], offs)
-        load_w(3, 0, 0)
-        load_x(1)
-
-        cw("s", 1, 0, 0)
-        cw("v", 1, 0, 1)
-        qw(1, 0, 0)
-        qw(1, 0, 1)
-        cx("v", 0, 0)
-        cx("s", 0, 1)
-        qx(0, 0)
-        cx("v", 0, 2)
-        qx(0, 1)
-        qx(0, 2)
-        gather(0)
-        cw("s", 3, 0, 0)
-        cx("s", 1, 0)
-        cx("v", 1, 1)
-        qw(3, 0, 0)
-        cx("s", 1, 2)
-        qx(1, 0)
-        qx(1, 1)
-        qx(1, 2)
-        load_w(3, 0, 1)
-        load_w(1, 1, 0)
-        cw("v", 3, 0, 1)
-        gather(1)
-        qw(3, 0, 1)
-        load_w2(0)
-        cw2("s", 0)
-        cw("s", 1, 1, 0)
-        mm(1, 0)
-        silu(0)
-        mm(3, 0)
-        qw2(0)
-        nc.sync.dma_start(gates[:], gate)
-
-        for e in range(1, E):
-            last = e == E - 1
-            load_w(1, e, 1)
-            if not last:
-                load_w2(e)
-            load_w(3, e, 0)
-            load_w(3, e, 1)
-            if last:
-                load_w2(e)
-            else:
-                load_w(1, e + 1, 0)
-            cw("v", 1, e, 1)
-            cw("s", 3, e, 0)
-            qw(1, e, 0)
-            mul(e - 1)
-            qw(1, e, 1)
-            mm(1, e)
-            qh(e - 1)
-            my(e - 1)
-            cy("s", e - 1)
-            silu(e)
-            if e == 4:
-                scatter(0, 384)
-            if e == 5:
-                scatter(384, 576)
-            if not last:
-                cw2("s", e)
-            if last:
-                cw("vs", 3, e, 1)
-                qw(3, e, 0)
-                qw(3, e, 1, 2)
-                cw2("s", e)
-                qw2(e)
-            else:
-                extra = "s" if e == 2 else "v"
-                cw(extra, 3, e, 1)
-                qw(3, e, 0)
-                qw(3, e, 1)
-                cw("s", 1, e + 1, 0)
-                qw2(e)
-            mm(3, e)
-        e = E - 1
-        mul(e)
-        qh(e)
-        my(e)
-        cy("s", e)
-        scatter(576, 768)
+        for s in LOADS_AND_STEPS:
+            k, a = s[0], s[1:]
+            if k == "lw":
+                load_w(*a)
+            elif k == "lx":
+                load_x(*a)
+            elif k == "lo":
+                nc.sync.dma_start(offsets[:], offs)
+            elif k == "lg":
+                nc.sync.dma_start(gates[:], gate)
+            elif k == "l2":
+                load_w2(*a)
+            elif k == "cw":
+                cw(*a)
+            elif k == "qw":
+                qw(*a)
+            elif k == "mm":
+                mm(*a)
+            elif k == "silu":
+                silu(*a)
+            elif k == "mul":
+                mul(*a)
+            elif k == "qh":
+                qh(*a)
+            elif k == "my":
+                my(*a)
+            elif k == "cy":
+                cy(*a)
+            elif k == "cx":
+                cx(*a)
+            elif k == "qx":
+                qx(*a)
+            elif k == "ga":
+                gather(*a)
+            elif k == "c2":
+                cw2(*a)
+            elif k == "q2":
+                qw2(*a)
+            elif k == "sc":
+                scatter(*a)
         nc.sync.dma_start(out, window[:])

@@ -13,23 +13,21 @@ U16 = mybir.dt.uint16
 U8 = mybir.dt.uint8
 FP8X4 = mybir.dt.float8_e4m3fn_x4
 SILU = mybir.ActivationFunctionType.Silu
+COPY = mybir.ActivationFunctionType.Copy
 MULT = mybir.AluOpType.mult
 
 LOADS_AND_STEPS = [
     ('lw', 1, 0, 0),
-    ('cw', 's', 1, 0, 0),
+    ('cw', 'vs', 1, 0, 0),
     ('lo',),
-    ('l2', 0),
-    ('c2', 'v', 0),
-    ('q2', 0),
     ('lx', 0),
     ('cx', 's', 0, 0),
     ('cx', 'v', 0, 1),
-    ('cx', 'v', 0, 2),
-    ('qx', 0, 0),
-    ('qx', 0, 1),
-    ('qx', 0, 2),
-    ('ga', 0),
+    ('cx', 's', 0, 2),
+    ('qt', 0, 0),
+    ('qt', 0, 1),
+    ('qt', 0, 2),
+    ('gb', 0),
     ('lw', 1, 0, 1),
     ('cw', 'vs', 1, 0, 1),
     ('qw', 1, 0),
@@ -37,120 +35,139 @@ LOADS_AND_STEPS = [
     ('cx', 's', 1, 0),
     ('cx', 'v', 1, 1),
     ('cx', 's', 1, 2),
-    ('qx', 1, 0),
-    ('qx', 1, 1),
-    ('qx', 1, 2),
-    ('ga', 1),
+    ('qt', 1, 0),
+    ('qt', 1, 1),
+    ('qt', 1, 2),
+    ('gb', 1),
     ('mm', 1, 0),
     ('silu', 0),
+    ('lw', 3, 2, 0),
+    ('cw', 'v', 3, 2, 0),
+    ('qw', 3, 2, 0, 512),
+    ('lw', 3, 2, 1),
+    ('cw', 's', 3, 2, 1),
+    ('qw', 3, 2, 512, 1024),
     ('lw', 3, 0, 0),
     ('cw', 'vs', 3, 0, 0),
-    ('lw', 1, 1, 0),
-    ('cw', 's', 1, 1, 0),
+    ('qw', 3, 0, 0, 512),
     ('lw', 3, 1, 0),
-    ('cw', 'sv', 3, 1, 0),
-    ('lw', 1, 1, 1),
-    ('cw', 'v', 1, 1, 1),
-    ('qw', 1, 1),
+    ('cw', 'vs', 3, 1, 0),
     ('lw', 3, 0, 1),
-    ('cw', 'v', 3, 0, 1),
-    ('qw', 3, 0),
+    ('cw', 'vs', 3, 0, 1),
+    ('qw', 3, 0, 512, 1024),
     ('mm', 3, 0),
+    ('lw', 3, 1, 1),
+    ('cw', 's', 3, 1, 1),
+    ('qw', 3, 1),
+    ('lw', 1, 1, 0),
+    ('cw', 'v', 1, 1, 0),
+    ('l2', 2),
+    ('c2', 's', 2),
+    ('q2', 2),
+    ('lw', 1, 2, 0),
+    ('cw', 'sv', 1, 2, 0),
+    ('qw', 1, 2, 0, 512),
+    ('lw', 1, 1, 1),
+    ('cw', 's', 1, 1, 1),
+    ('qw', 1, 1),
     ('mm', 1, 1),
     ('silu', 1),
-    ('lw', 3, 1, 1),
-    ('cw', 'vs', 3, 1, 1),
-    ('qw', 3, 1),
     ('mm', 3, 1),
-    ('lg',),
-    ('lw', 1, 2, 0),
-    ('cw', 's', 1, 2, 0),
+    ('l2', 0),
+    ('c2', 's', 0),
+    ('q2', 0),
+    ('lw', 1, 3, 0),
+    ('cw', 'sv', 1, 3, 0),
+    ('qw', 1, 3, 0, 512),
+    ('lg', 384, 768),
+    ('lw', 3, 3, 0),
+    ('cw', 'sv', 3, 3, 0),
+    ('lg', 0, 384),
     ('lw', 1, 2, 1),
-    ('cw', 's', 1, 2, 1),
-    ('qw', 1, 2),
+    ('cw', 'v', 1, 2, 1),
+    ('qw', 1, 2, 512, 1024),
     ('mm', 1, 2),
     ('silu', 2),
+    ('mm', 3, 2),
     ('l2', 1),
-    ('c2', 's', 1),
+    ('c2', 'v', 1),
     ('q2', 1),
     ('mul', 0, 0, 2),
     ('mul', 1, 1, 2),
     ('qh', (0, 1)),
     ('my', (0, 1)),
     ('cy', 's', (0, 1)),
-    ('sc', 0, 256),
-    ('lw', 3, 2, 0),
-    ('cw', 's', 3, 2, 0),
-    ('l2', 2),
-    ('c2', 'v', 2),
-    ('q2', 2),
-    ('lw', 3, 2, 1),
-    ('cw', 'v', 3, 2, 1),
-    ('qw', 3, 2),
-    ('mm', 3, 2),
-    ('lw', 1, 3, 0),
-    ('cw', 'v', 1, 3, 0),
-    ('lw', 1, 3, 1),
-    ('cw', 's', 1, 3, 1),
-    ('qw', 1, 3),
-    ('mm', 1, 3),
-    ('silu', 3),
-    ('lw', 3, 3, 0),
-    ('cw', 's', 3, 3, 0),
+    ('mul', 2, 0, 1),
+    ('qh', (2,)),
+    ('my', (2,)),
+    ('cy', 's', (2,)),
+    ('sc', 0, 384),
     ('lw', 3, 3, 1),
     ('cw', 'v', 3, 3, 1),
     ('qw', 3, 3),
+    ('lw', 1, 3, 1),
+    ('cw', 's', 1, 3, 1),
+    ('qw', 1, 3, 512, 1024),
+    ('mm', 1, 3),
+    ('silu', 3),
     ('mm', 3, 3),
+    ('lw', 3, 4, 0),
+    ('cw', 'sv', 3, 4, 0),
+    ('l2', 4),
+    ('c2', 's', 4),
+    ('q2', 4),
+    ('lw', 3, 4, 1),
+    ('cw', 'sv', 3, 4, 1),
+    ('qw', 3, 4),
     ('lw', 1, 4, 0),
-    ('cw', 'vs', 1, 4, 0),
-    ('l2', 3),
-    ('c2', 'v', 3),
-    ('q2', 3),
-    ('mul', 2, 0, 2),
-    ('mul', 3, 1, 2),
-    ('qh', (2, 3)),
-    ('my', (2, 3)),
-    ('cy', 's', (2, 3)),
-    ('sc', 256, 512),
+    ('cw', 'sv', 1, 4, 0),
+    ('qw', 1, 4, 0, 512),
     ('lw', 1, 4, 1),
-    ('cw', 'sv', 1, 4, 1),
-    ('qw', 1, 4),
+    ('cw', 's', 1, 4, 1),
+    ('qw', 1, 4, 512, 1024),
     ('mm', 1, 4),
     ('silu', 4),
-    ('lw', 3, 4, 0),
-    ('cw', 's', 3, 4, 0),
-    ('lw', 3, 4, 1),
-    ('cw', 'v', 3, 4, 1),
-    ('qw', 3, 4),
     ('mm', 3, 4),
-    ('l2', 4),
-    ('c2', 'v', 4),
-    ('q2', 4),
-    ('lw', 3, 5, 0),
-    ('cw', 'v', 3, 5, 0),
-    ('qw', 3, 5, 0, 512),
     ('lw', 1, 5, 0),
-    ('cw', 's', 1, 5, 0),
+    ('cw', 'sv', 1, 5, 0),
+    ('qw', 1, 5, 0, 512),
+    ('lw', 3, 5, 0),
+    ('cw', 'sv', 3, 5, 0),
+    ('qw', 3, 5, 0, 512),
     ('lw', 1, 5, 1),
-    ('cw', 'v', 1, 5, 1),
-    ('qw', 1, 5),
+    ('cw', 'vs', 1, 5, 1),
+    ('qw', 1, 5, 512, 1024),
     ('mm', 1, 5),
     ('silu', 5),
-    ('lw', 3, 5, 1),
-    ('cw', 'vs', 3, 5, 1),
+    ('lwh', 3, 5, 1, 0),
+    ('cwh', 's', 3, 5, 1, 0),
+    ('lwh', 3, 5, 1, 1),
+    ('cwh', 'v', 3, 5, 1, 1),
     ('qw', 3, 5, 512, 768),
     ('qw', 3, 5, 768, 1024),
     ('mm', 3, 5),
+    ('l2', 3),
+    ('c2', 'v', 3),
+    ('q2', 3),
+    ('mul', 3, 0, 1),
+    ('qh', (3,)),
+    ('my', (3,)),
+    ('cy', 's', (3,)),
+    ('mul', 4, 0, 1),
+    ('qh', (4,)),
+    ('my', (4,)),
+    ('cy', 's', (4,)),
+    ('sc', 384, 576),
     ('l2', 5, 'ring'),
     ('c2', 's', 5),
     ('q2', 5),
-    ('mul', 4, 0, 2),
-    ('mul', 5, 1, 2),
-    ('qh', (4, 5)),
-    ('my', (4, 5)),
-    ('cy', 'v', (4, 5)),
-    ('sc', 512, 768),
+    ('mul', 5, 0, 1),
+    ('qh', (5,)),
+    ('my', (5,)),
+    ('cy', 's', (5,)),
+    ('sc', 576, 768),
 ]
+XMODE = ['b', 'b']
 
 P = 128
 J = 4
@@ -163,7 +180,7 @@ def tile_routed_moe_kernel(tc, xT, w1, w3, w2, gate, offs, out):
     nc = tc.nc
     with ExitStack() as ctx:
         keep = ctx.enter_context(tc.tile_pool(name="keep", bufs=1))
-        ring = ctx.enter_context(tc.tile_pool(name="ring", bufs=7))
+        ring = ctx.enter_context(tc.tile_pool(name="ring", bufs=8))
         two = ctx.enter_context(tc.tile_pool(name="two", bufs=2))
         three = ctx.enter_context(tc.tile_pool(name="three", bufs=3))
         pair = ctx.enter_context(tc.tile_pool(name="pair", bufs=2))
@@ -189,6 +206,22 @@ def tile_routed_moe_kernel(tc, xT, w1, w3, w2, gate, offs, out):
             nc.sync.dma_start(r[:], weight[l][e, g * KP:(g + 1) * KP, :].rearrange("(p j) c -> p (j c)", j=J))
             raw[l, e, g] = r
 
+        def load_wh(l, e, g, h):
+            if h == 0:
+                raw[l, e, g] = ring.tile([P, J * H], F32, name="raw", tag="raw")
+            rows = weight[l][e, g * KP:(g + 1) * KP, :].rearrange("(p j) c -> p j c", j=J)
+            nc.sync.dma_start(raw[l, e, g][:, h * 2 * H:(h + 1) * 2 * H].rearrange("p (j c) -> p j c", j=2), rows[:, 2 * h:2 * h + 2, :])
+
+        def cwh(eng, l, e, g, h):
+            t = grp[l, e][:, g * J * H:(g + 1) * J * H]
+            dst = t.rearrange("p (t m j) -> p m j t", t=J, j=J)[:, :, 2 * h:2 * h + 2, :]
+            src = raw[l, e, g][:, h * 2 * H:(h + 1) * 2 * H].rearrange("p (j m t) -> p m j t", j=2, t=J)
+            if len(eng) == 1:
+                copy(eng, dst, src)
+            else:
+                copy(eng[0], dst[:, :, :, 0:2], src[:, :, :, 0:2])
+                copy(eng[1], dst[:, :, :, 2:4], src[:, :, :, 2:4])
+
         def load_w2(e, pool_name="two"):
             pool, tag = (two, "w2raw") if pool_name == "two" else (ring, "raw")
             r = pool.tile([P, J * N], F32, name=tag, tag=tag)
@@ -197,9 +230,7 @@ def tile_routed_moe_kernel(tc, xT, w1, w3, w2, gate, offs, out):
 
         def load_x(g):
             r = keep.tile([P, J * T], F32, name="xraw%d" % g)
-            rows = xT[g * KP:(g + 1) * KP, :].rearrange("(p j) n -> p j n", j=J)
-            for j in range(J):
-                nc.sync.dma_start(r[:, j * T:(j + 1) * T], rows[:, j, :])
+            nc.sync.dma_start(r[:], xT[g * KP:(g + 1) * KP, :].rearrange("(p j) n -> p (j n)", j=J))
             raw["x", g] = r
 
         def copy(eng, dst, src):
@@ -217,11 +248,17 @@ def tile_routed_moe_kernel(tc, xT, w1, w3, w2, gate, offs, out):
             t = grp[l, e][:, g * J * H:(g + 1) * J * H]
             dst = t.rearrange("p (t m j) -> p m j t", t=J, j=J)
             src = raw[l, e, g][:].rearrange("p (j m t) -> p m j t", j=J, t=J)
-            if len(eng) == 1:
-                copy(eng, dst, src)
-            else:
-                for h in range(2):
-                    copy(eng[h], dst[:, :, :, 2 * h:2 * h + 2], src[:, :, :, 2 * h:2 * h + 2])
+            full = "".join(c * (J // len(eng)) for c in eng)
+            a = 0
+            while a < J:
+                b = a
+                while b < J and full[b] == full[a]:
+                    b += 1
+                if b - a == J:
+                    copy(full[a], dst, src)
+                else:
+                    copy(full[a], dst[:, :, :, a:b], src[:, :, :, a:b])
+                a = b
 
         def qw(l, e, a=0, b=G * H):
             if a == 0:
@@ -241,24 +278,54 @@ def tile_routed_moe_kernel(tc, xT, w1, w3, w2, gate, offs, out):
             codes[2, e], scales[2, e] = code, scale
 
         def cx(eng, g, b):
-            cols = slice(b * XB, (b + 1) * XB)
-            t = three.tile([P, XB, J], BF16, name="xgrp", tag="xgrp", align_bytes=64)
             rows = raw["x", g][:].rearrange("p (j n) -> p j n", j=J)
-            copy(eng, t[:].rearrange("p (c i) j -> p c j i", i=4), rows[:, :, cols].rearrange("p j (c i) -> p c j i", i=4))
-            grp["x", g, b] = t
+            if XMODE[g] == "b":
+                cols = slice(b * XB, (b + 1) * XB)
+                t = three.tile([P, XB, J], BF16, name="xgrp", tag="xgrp", align_bytes=64)
+                copy(eng, t[:].rearrange("p (c i) j -> p c j i", i=4), rows[:, :, cols].rearrange("p j (c i) -> p c j i", i=4))
+                grp["x", g, b] = t
+            elif XMODE[g] == "f":
+                t = keep.tile([P, T], BF16, name="xb%d%d" % (g, b), align_bytes=64)
+                grp["x", g, b] = t
+                copy(eng, t[:], rows[:, b, :])
+            else:
+                u, h = b // 2, b % 2
+                if h == 0:
+                    grp["x", g, u] = keep.tile([P, T * 2], BF16, name="xp%d%d" % (g, u), align_bytes=64)
+                t = grp["x", g, u][:, h * T:(h + 1) * T]
+                copy(eng, t.rearrange("p (c i j) -> p c j i", i=4, j=2),
+                     rows[:, 2 * u:2 * u + 2, h * T // 2:(h + 1) * T // 2].rearrange("p j (c i) -> p c j i", i=4))
 
-        def qx(g, b):
+        def ga(g, b):
+            if b == 0:
+                grp["g", g] = keep.tile([P, S * J], BF16, name="xg%d" % g, align_bytes=64)
+            t = grp["g", g][:]
+            if XMODE[g] == "f":
+                nc.scalar.activation(t.rearrange("p (n j) -> p n j", j=J)[:, :, b], grp["x", g, b][:].indirect(offsets[:]), COPY)
+            else:
+                nc.vector.tensor_copy(t.bitcast(U32).rearrange("p (n u) -> p n u", u=2)[:, :, b],
+                                      grp["x", g, b][:].bitcast(U32).indirect(offsets[:]))
+
+        xcode, xscale = {}, {}
+
+        def qt(g, b):
+            if b == 0:
+                xcode[g] = keep.tile([P, T], U32, name="xc%d" % g, align_bytes=64)
+                xscale[g] = keep.tile([P, T], U8, name="xs%d" % g, align_bytes=64)
             cols = slice(b * XB, (b + 1) * XB)
             quant(xcode[g][:, cols], xscale[g][:, cols], grp["x", g, b][:].rearrange("p n j -> p (n j)"))
 
-        xcode = [keep.tile([P, T], U32, name="xc%d" % g, align_bytes=64) for g in range(G)]
-        xscale = [keep.tile([P, T], U8, name="xs%d" % g, align_bytes=64) for g in range(G)]
-
-        def gather(g):
+        def gb(g):
             gc[g] = keep.tile([P, S], U32, name="gc%d" % g, align_bytes=64)
             gs[g] = keep.tile([P, S], U8, name="gs%d" % g, align_bytes=64)
             nc.vector.tensor_copy(gc[g][:], xcode[g][:].indirect(offsets[:]))
             nc.vector.tensor_copy(gs[g][:], xscale[g][:].indirect(offsets[:]))
+
+        def qx(g):
+            gc[g] = keep.tile([P, S], U32, name="gc%d" % g, align_bytes=64)
+            gs[g] = keep.tile([P, S], U8, name="gs%d" % g, align_bytes=64)
+            for a, b in ((0, 512), (512, 768)):
+                quant(gc[g][:, a:b], gs[g][:, a:b], grp["g", g][:, J * a:J * b])
 
         def mm(l, e):
             a = psum.tile([P, J, C], F32, name="acc%d" % l, tag="acc%d" % l)
@@ -317,7 +384,7 @@ def tile_routed_moe_kernel(tc, xT, w1, w3, w2, gate, offs, out):
             elif k == "lo":
                 nc.sync.dma_start(offsets[:], offs)
             elif k == "lg":
-                nc.sync.dma_start(gates[:], gate)
+                nc.sync.dma_start(gates[:, a[0]:a[1]], gate[:, a[0]:a[1]])
             elif k == "l2":
                 load_w2(*a)
             elif k == "cw":
@@ -340,8 +407,16 @@ def tile_routed_moe_kernel(tc, xT, w1, w3, w2, gate, offs, out):
                 cx(*a)
             elif k == "qx":
                 qx(*a)
+            elif k == "qt":
+                qt(*a)
+            elif k == "gb":
+                gb(*a)
+            elif k == "lwh":
+                load_wh(*a)
+            elif k == "cwh":
+                cwh(*a)
             elif k == "ga":
-                gather(*a)
+                ga(*a)
             elif k == "c2":
                 cw2(*a)
             elif k == "q2":

from contextlib import ExitStack

import concourse.mybir as mybir

K, T, E, C, H, N = 1024, 1536, 6, 128, 512, 128
S = E * C
FLOPS = 2 * (2 * S * K * H) + 2 * S * H * N

F32 = mybir.dt.float32
BF16 = mybir.dt.bfloat16
U32 = mybir.dt.uint32
U16 = mybir.dt.uint16
U8 = mybir.dt.uint8
FP8X4 = mybir.dt.float8_e4m3fn_x4
SILU = mybir.ActivationFunctionType.Silu
COPY = mybir.ActivationFunctionType.Copy
MULT = mybir.AluOpType.mult

LOADS_AND_STEPS = [
    ('lw', 1, 0, 0),
    ('cw', 'vs', 1, 0, 0),
    ('lo',),
    ('lx', 0),
    ('cx', 's', 0, 0),
    ('cx', 'v', 0, 1),
    ('cx', 's', 0, 2),
    ('qt', 0, 0),
    ('qt', 0, 1),
    ('qt', 0, 2),
    ('gb', 0),
    ('lw', 1, 0, 1),
    ('cw', 'vs', 1, 0, 1),
    ('qw', 1, 0),
    ('lx', 1),
    ('cx', 's', 1, 0),
    ('cx', 'v', 1, 1),
    ('cx', 's', 1, 2),
    ('qt', 1, 0),
    ('qt', 1, 1),
    ('qt', 1, 2),
    ('gb', 1),
    ('mm', 1, 0),
    ('silu', 0),
    ('lw', 3, 2, 0),
    ('cw', 'v', 3, 2, 0),
    ('qw', 3, 2, 0, 512),
    ('lw', 3, 2, 1),
    ('cw', 's', 3, 2, 1),
    ('qw', 3, 2, 512, 1024),
    ('lw', 3, 0, 0),
    ('cw', 'vs', 3, 0, 0),
    ('qw', 3, 0, 0, 512),
    ('lw', 3, 1, 0),
    ('cw', 'vs', 3, 1, 0),
    ('lw', 3, 0, 1),
    ('cw', 'vs', 3, 0, 1),
    ('qw', 3, 0, 512, 1024),
    ('mm', 3, 0),
    ('lw', 3, 1, 1),
    ('cw', 's', 3, 1, 1),
    ('qw', 3, 1),
    ('lw', 1, 1, 0),
    ('cw', 'v', 1, 1, 0),
    ('l2', 2),
    ('c2', 's', 2),
    ('q2', 2),
    ('lw', 1, 2, 0),
    ('cw', 'sv', 1, 2, 0),
    ('qw', 1, 2, 0, 512),
    ('lw', 1, 1, 1),
    ('cw', 's', 1, 1, 1),
    ('qw', 1, 1),
    ('mm', 1, 1),
    ('silu', 1),
    ('mm', 3, 1),
    ('l2', 0),
    ('c2', 's', 0),
    ('q2', 0),
    ('lw', 1, 3, 0),
    ('cw', 'sv', 1, 3, 0),
    ('qw', 1, 3, 0, 512),
    ('lg', 384, 768),
    ('lw', 3, 3, 0),
    ('cw', 'sv', 3, 3, 0),
    ('lg', 0, 384),
    ('lw', 1, 2, 1),
    ('cw', 'v', 1, 2, 1),
    ('qw', 1, 2, 512, 1024),
    ('mm', 1, 2),
    ('silu', 2),
    ('mm', 3, 2),
    ('l2', 1),
    ('c2', 'v', 1),
    ('q2', 1),
    ('mul', 0, 0, 2),
    ('mul', 1, 1, 2),
    ('qh', (0, 1)),
    ('my', (0, 1)),
    ('cy', 's', (0, 1)),
    ('mul', 2, 0, 1),
    ('qh', (2,)),
    ('my', (2,)),
    ('cy', 's', (2,)),
    ('sc', 0, 384),
    ('lw', 3, 3, 1),
    ('cw', 'v', 3, 3, 1),
    ('qw', 3, 3),
    ('lw', 1, 3, 1),
    ('cw', 's', 1, 3, 1),
    ('qw', 1, 3, 512, 1024),
    ('mm', 1, 3),
    ('silu', 3),
    ('mm', 3, 3),
    ('lw', 3, 4, 0),
    ('cw', 'sv', 3, 4, 0),
    ('l2', 4),
    ('c2', 's', 4),
    ('q2', 4),
    ('lw', 3, 4, 1),
    ('cw', 'sv', 3, 4, 1),
    ('qw', 3, 4),
    ('lw', 1, 4, 0),
    ('cw', 'sv', 1, 4, 0),
    ('qw', 1, 4, 0, 512),
    ('lw', 1, 4, 1),
    ('cw', 's', 1, 4, 1),
    ('qw', 1, 4, 512, 1024),
    ('mm', 1, 4),
    ('silu', 4),
    ('mm', 3, 4),
    ('lw', 1, 5, 0),
    ('cw', 'sv', 1, 5, 0),
    ('qw', 1, 5, 0, 512),
    ('lw', 3, 5, 0),
    ('cw', 'sv', 3, 5, 0),
    ('qw', 3, 5, 0, 512),
    ('lw', 1, 5, 1),
    ('cw', 'vs', 1, 5, 1),
    ('qw', 1, 5, 512, 1024),
    ('mm', 1, 5),
    ('silu', 5),
    ('lwh', 3, 5, 1, 0),
    ('cwh', 's', 3, 5, 1, 0),
    ('lwh', 3, 5, 1, 1),
    ('cwh', 'v', 3, 5, 1, 1),
    ('qw', 3, 5, 512, 768),
    ('qw', 3, 5, 768, 1024),
    ('mm', 3, 5),
    ('l2', 3),
    ('c2', 'v', 3),
    ('q2', 3),
    ('mul', 3, 0, 1),
    ('qh', (3,)),
    ('my', (3,)),
    ('cy', 's', (3,)),
    ('mul', 4, 0, 1),
    ('qh', (4,)),
    ('my', (4,)),
    ('cy', 's', (4,)),
    ('sc', 384, 576),
    ('l2', 5, 'ring'),
    ('c2', 's', 5),
    ('q2', 5),
    ('mul', 5, 0, 1),
    ('qh', (5,)),
    ('my', (5,)),
    ('cy', 's', (5,)),
    ('sc', 576, 768),
]
XMODE = ['b', 'b']

P = 128
J = 4
KP = P * J
G = K // KP
XB = 512


def tile_routed_moe_kernel(tc, xT, w1, w3, w2, gate, offs, out):
    nc = tc.nc
    with ExitStack() as ctx:
        keep = ctx.enter_context(tc.tile_pool(name="keep", bufs=1))
        ring = ctx.enter_context(tc.tile_pool(name="ring", bufs=8))
        two = ctx.enter_context(tc.tile_pool(name="two", bufs=2))
        three = ctx.enter_context(tc.tile_pool(name="three", bufs=3))
        pair = ctx.enter_context(tc.tile_pool(name="pair", bufs=2))
        cpool = ctx.enter_context(tc.tile_pool(name="cpool", bufs=2))
        psum = ctx.enter_context(tc.psum_pool(name="psum", bufs=2))

        offsets = keep.tile([P, S // 16], U16, name="offsets")
        window = keep.tile([P, T], F32, name="window")
        y_all = keep.tile([P, S], F32, name="y_all")
        gates = keep.tile([P, S], F32, name="gates")
        warm = keep.tile([P, 8], F32, name="warm")

        nc.gpsimd.memset(warm[:], 0.0)
        nc.gpsimd.memset(window[:], 0.0)
        nc.scalar.activation(warm[:, 0:1], warm[:, 1:2], SILU)

        raw, grp, codes, scales = {}, {}, {}, {}
        acc, act, hid, hcode, hscale, gc, gs = {}, {}, {}, {}, {}, {}, {}
        weight = {1: w1, 3: w3}

        def load_w(l, e, g):
            r = ring.tile([P, J * H], F32, name="raw", tag="raw")
            nc.sync.dma_start(r[:], weight[l][e, g * KP:(g + 1) * KP, :].rearrange("(p j) c -> p (j c)", j=J))
            raw[l, e, g] = r

        def load_wh(l, e, g, h):
            if h == 0:
                raw[l, e, g] = ring.tile([P, J * H], F32, name="raw", tag="raw")
            rows = weight[l][e, g * KP:(g + 1) * KP, :].rearrange("(p j) c -> p j c", j=J)
            nc.sync.dma_start(raw[l, e, g][:, h * 2 * H:(h + 1) * 2 * H].rearrange("p (j c) -> p j c", j=2), rows[:, 2 * h:2 * h + 2, :])

        def cwh(eng, l, e, g, h):
            t = grp[l, e][:, g * J * H:(g + 1) * J * H]
            dst = t.rearrange("p (t m j) -> p m j t", t=J, j=J)[:, :, 2 * h:2 * h + 2, :]
            src = raw[l, e, g][:, h * 2 * H:(h + 1) * 2 * H].rearrange("p (j m t) -> p m j t", j=2, t=J)
            if len(eng) == 1:
                copy(eng, dst, src)
            else:
                copy(eng[0], dst[:, :, :, 0:2], src[:, :, :, 0:2])
                copy(eng[1], dst[:, :, :, 2:4], src[:, :, :, 2:4])

        def load_w2(e, pool_name="two"):
            pool, tag = (two, "w2raw") if pool_name == "two" else (ring, "raw")
            r = pool.tile([P, J * N], F32, name=tag, tag=tag)
            nc.sync.dma_start(r[:], w2[e].rearrange("(p j) n -> p (j n)", j=J))
            raw[2, e] = r

        def load_x(g):
            r = keep.tile([P, J * T], F32, name="xraw%d" % g)
            nc.sync.dma_start(r[:], xT[g * KP:(g + 1) * KP, :].rearrange("(p j) n -> p (j n)", j=J))
            raw["x", g] = r

        def copy(eng, dst, src):
            if eng == "v":
                nc.vector.tensor_copy(out=dst, in_=src)
            else:
                nc.scalar.copy(dst, src)

        def quant(code, scale, src):
            nc.vector.quantize_mx(out=code.bitcast(FP8X4), scales=scale, in_=src)

        def cw(eng, l, e, g):
            if g == 0:
                grp[l, e] = pair.tile([P, G * J * H], BF16, name="wgrp", tag="wgrp", align_bytes=64)
            t = grp[l, e][:, g * J * H:(g + 1) * J * H]
            dst = t.rearrange("p (t m j) -> p m j t", t=J, j=J)
            src = raw[l, e, g][:].rearrange("p (j m t) -> p m j t", j=J, t=J)
            full = "".join(c * (J // len(eng)) for c in eng)
            a = 0
            while a < J:
                b = a
                while b < J and full[b] == full[a]:
                    b += 1
                if b - a == J:
                    copy(full[a], dst, src)
                else:
                    copy(full[a], dst[:, :, :, a:b], src[:, :, :, a:b])
                a = b

        def qw(l, e, a=0, b=G * H):
            if a == 0:
                codes[l, e] = cpool.tile([P, G * H], U32, name="c%d" % l, tag="c%d" % l, align_bytes=64)
                scales[l, e] = cpool.tile([P, G * H], U8, name="s%d" % l, tag="s%d" % l, align_bytes=64)
            quant(codes[l, e][:, a:b], scales[l, e][:, a:b], grp[l, e][:, J * a:J * b])

        def cw2(eng, e):
            t = two.tile([P, N, J], BF16, name="w2grp", tag="w2grp", align_bytes=64)
            copy(eng, t[:].rearrange("p (c i) j -> p c j i", i=4), raw[2, e][:].rearrange("p (j c i) -> p c j i", j=J, i=4))
            grp[2, e] = t

        def qw2(e):
            code = three.tile([P, N], U32, name="c2", tag="c2", align_bytes=64)
            scale = three.tile([P, N], U8, name="s2", tag="s2", align_bytes=64)
            quant(code[:], scale[:], grp[2, e][:].rearrange("p n j -> p (n j)"))
            codes[2, e], scales[2, e] = code, scale

        def cx(eng, g, b):
            rows = raw["x", g][:].rearrange("p (j n) -> p j n", j=J)
            if XMODE[g] == "b":
                cols = slice(b * XB, (b + 1) * XB)
                t = three.tile([P, XB, J], BF16, name="xgrp", tag="xgrp", align_bytes=64)
                copy(eng, t[:].rearrange("p (c i) j -> p c j i", i=4), rows[:, :, cols].rearrange("p j (c i) -> p c j i", i=4))
                grp["x", g, b] = t
            elif XMODE[g] == "f":
                t = keep.tile([P, T], BF16, name="xb%d%d" % (g, b), align_bytes=64)
                grp["x", g, b] = t
                copy(eng, t[:], rows[:, b, :])
            else:
                u, h = b // 2, b % 2
                if h == 0:
                    grp["x", g, u] = keep.tile([P, T * 2], BF16, name="xp%d%d" % (g, u), align_bytes=64)
                t = grp["x", g, u][:, h * T:(h + 1) * T]
                copy(eng, t.rearrange("p (c i j) -> p c j i", i=4, j=2),
                     rows[:, 2 * u:2 * u + 2, h * T // 2:(h + 1) * T // 2].rearrange("p j (c i) -> p c j i", i=4))

        def ga(g, b):
            if b == 0:
                grp["g", g] = keep.tile([P, S * J], BF16, name="xg%d" % g, align_bytes=64)
            t = grp["g", g][:]
            if XMODE[g] == "f":
                nc.scalar.activation(t.rearrange("p (n j) -> p n j", j=J)[:, :, b], grp["x", g, b][:].indirect(offsets[:]), COPY)
            else:
                nc.vector.tensor_copy(t.bitcast(U32).rearrange("p (n u) -> p n u", u=2)[:, :, b],
                                      grp["x", g, b][:].bitcast(U32).indirect(offsets[:]))

        xcode, xscale = {}, {}

        def qt(g, b):
            if b == 0:
                xcode[g] = keep.tile([P, T], U32, name="xc%d" % g, align_bytes=64)
                xscale[g] = keep.tile([P, T], U8, name="xs%d" % g, align_bytes=64)
            cols = slice(b * XB, (b + 1) * XB)
            quant(xcode[g][:, cols], xscale[g][:, cols], grp["x", g, b][:].rearrange("p n j -> p (n j)"))

        def gb(g):
            gc[g] = keep.tile([P, S], U32, name="gc%d" % g, align_bytes=64)
            gs[g] = keep.tile([P, S], U8, name="gs%d" % g, align_bytes=64)
            nc.vector.tensor_copy(gc[g][:], xcode[g][:].indirect(offsets[:]))
            nc.vector.tensor_copy(gs[g][:], xscale[g][:].indirect(offsets[:]))

        def qx(g):
            gc[g] = keep.tile([P, S], U32, name="gc%d" % g, align_bytes=64)
            gs[g] = keep.tile([P, S], U8, name="gs%d" % g, align_bytes=64)
            for a, b in ((0, 512), (512, 768)):
                quant(gc[g][:, a:b], gs[g][:, a:b], grp["g", g][:, J * a:J * b])

        def mm(l, e):
            a = psum.tile([P, J, C], F32, name="acc%d" % l, tag="acc%d" % l)
            cols = slice(e * C, (e + 1) * C)
            for t in range(J):
                for g in range(G):
                    nc.tensor.matmul_mx(
                        out=a[:, t, :],
                        lhsT=codes[l, e][:, g * H + t * P:g * H + (t + 1) * P].bitcast(FP8X4),
                        lhsT_scale=scales[l, e][:, g * H + t * P:g * H + (t + 1) * P],
                        rhs=gc[g][:, cols].bitcast(FP8X4),
                        rhs_scale=gs[g][:, cols],
                        start=(g == 0),
                        stop=(g == G - 1),
                    )
            acc[l, e] = a

        def silu(e):
            act[e] = two.tile([P, J, C], F32, name="act")
            nc.scalar.activation(act[e][:], acc[1, e][:], SILU)

        def mul(e, i, n):
            if i == 0:
                hid[e] = two.tile([P, n * C, J], BF16, name="hid%d" % n, tag="hid%d" % n, align_bytes=64)
                hid["n"] = hid[e]
            h = hid["n"][:, i * C:(i + 1) * C, :]
            nc.vector.tensor_tensor(h, acc[3, e][:].rearrange("p t n -> p n t"), act[e][:].rearrange("p t n -> p n t"), MULT)

        def qh(es):
            n = len(es)
            hcode[es] = two.tile([P, n * C], U32, name="hc%d" % n, tag="hc%d" % n, align_bytes=64)
            hscale[es] = two.tile([P, n * C], U8, name="hs%d" % n, tag="hs%d" % n, align_bytes=64)
            quant(hcode[es][:], hscale[es][:], hid["n"][:].rearrange("p n t -> p (n t)"))

        def my(es):
            n = len(es)
            a = psum.tile([P, n * C], F32, name="accy", tag="accy")
            for i, e in enumerate(es):
                cols = slice(i * C, (i + 1) * C)
                nc.tensor.matmul_mx(out=a[:, cols], lhsT=codes[2, e][:].bitcast(FP8X4), lhsT_scale=scales[2, e][:],
                                    rhs=hcode[es][:, cols].bitcast(FP8X4), rhs_scale=hscale[es][:, cols], start=True, stop=True)
            acc["y", es] = a

        def cy(eng, es):
            copy(eng, y_all[:, es[0] * C:(es[-1] + 1) * C], acc["y", es][:])

        def scatter(a, b):
            nc.vector.tensor_tensor(window[:].indirect(offsets[:, a // 16:b // 16]), y_all[:, a:b], gates[:, a:b], MULT)

        for s in LOADS_AND_STEPS:
            k, a = s[0], s[1:]
            if k == "lw":
                load_w(*a)
            elif k == "lx":
                load_x(*a)
            elif k == "lo":
                nc.sync.dma_start(offsets[:], offs)
            elif k == "lg":
                nc.sync.dma_start(gates[:, a[0]:a[1]], gate[:, a[0]:a[1]])
            elif k == "l2":
                load_w2(*a)
            elif k == "cw":
                cw(*a)
            elif k == "qw":
                qw(*a)
            elif k == "mm":
                mm(*a)
            elif k == "silu":
                silu(*a)
            elif k == "mul":
                mul(*a)
            elif k == "qh":
                qh(*a)
            elif k == "my":
                my(*a)
            elif k == "cy":
                cy(*a)
            elif k == "cx":
                cx(*a)
            elif k == "qx":
                qx(*a)
            elif k == "qt":
                qt(*a)
            elif k == "gb":
                gb(*a)
            elif k == "lwh":
                load_wh(*a)
            elif k == "cwh":
                cwh(*a)
            elif k == "ga":
                ga(*a)
            elif k == "c2":
                cw2(*a)
            elif k == "q2":
                qw2(*a)
            elif k == "sc":
                scatter(*a)
        nc.sync.dma_start(out, window[:])
